import numpy as np
import ml_dtypes


def mxq(x, axis, fmt="e4m3"):
    dtype, down = {"e4m3": (ml_dtypes.float8_e4m3fn, 7), "e5m2": (ml_dtypes.float8_e5m2, 14)}[fmt]
    v = np.moveaxis(np.asarray(x, np.float32).astype(ml_dtypes.bfloat16).astype(np.float64), axis, -1)
    blocks = v.reshape(v.shape[:-1] + (-1, 32))
    amax = np.abs(blocks).max(-1, keepdims=True)
    byte = np.maximum(np.where(amax > 0, np.frexp(amax)[1] - 1 + 127, 0) - down, 1)
    scale = np.exp2(byte - 127.0)
    codes = (blocks / scale).astype(np.float32).astype(dtype).astype(np.float64)
    return np.moveaxis((codes * scale).reshape(v.shape), -1, axis)


WIDE = False


def mx_kscale(k):
    if not WIDE:
        return np.ones(k)
    levels = np.array([30, -30])
    if k % 512:
        return np.exp2(np.random.permutation(np.resize(levels, k // 32))).repeat(32)
    a = np.empty((k // 512, 16))
    for p in range(k // 512):
        a[p, :8] = np.random.permutation(np.resize(levels, 8))
        for g in range(8):
            far = levels[np.abs(levels - a[p, g]) >= 10]
            a[p, g + 8] = far[np.random.randint(len(far))]
    return np.exp2(a.ravel()).repeat(32)


def f64(x):
    return np.asarray(x).astype(np.float64)


def striped(idx):
    return np.tile(np.asarray(idx).reshape(-1, 16).T, (8, 1)).astype(np.uint16)


def unstriped(offs):
    return offs[:16].T.reshape(-1).astype(np.int64)


def striped8(idx):
    return np.asarray(idx).reshape(8, -1, 16).transpose(0, 2, 1).reshape(128, -1).astype(np.uint16)


def unstriped8(offs):
    return offs.reshape(8, 16, -1).transpose(0, 2, 1).reshape(8, -1).astype(np.int64)


def pick8(x, idx, run):
    r = np.arange(len(x))
    return x[r[:, None], idx[r % (8 * run) // run]]


E2M1 = np.array([0.0, 0.5, 1.0, 1.5, 2.0, 3.0, 4.0, 6.0, -0.0, -0.5, -1.0, -1.5, -2.0, -3.0, -4.0, -6.0])


def pack_weight(w, fmt):
    k, n = w.shape
    w = f64(np.asarray(w, np.float32).astype(ml_dtypes.bfloat16)).reshape(k // 32, 32, n)
    amax = np.abs(w).max(1)
    if fmt in ("e4m3", "e5m2"):
        byte = np.frexp(amax)[1] - 1 + 127 - (7 if fmt == "e4m3" else 14)
    else:
        mant, ex = np.frexp(amax / 6.0)
        byte = np.where(mant > 0.5, ex, ex - 1) + 127
    byte = np.clip(np.where(amax > 0, byte, 1), 1, 254)
    scaled = (w * np.exp2(127.0 - byte)[:, None, :]).reshape(k, n).astype(np.float32)
    by_word = np.ascontiguousarray(scaled.reshape(k // 512, 128, 4, n).transpose(0, 1, 3, 2))
    if fmt in ("e4m3", "e5m2"):
        words = by_word.astype(ml_dtypes.float8_e4m3fn if fmt == "e4m3" else ml_dtypes.float8_e5m2).view(np.uint8)
    else:
        c = by_word.astype(ml_dtypes.float4_e2m1fn).view(np.uint8) & 0xF
        words = (c[..., 0::2] | (c[..., 1::2] << 4)).reshape(k // 512, 128, 2 * n)
    return np.ascontiguousarray(words), np.ascontiguousarray(byte.astype(np.uint8).reshape(k // 512, 16, n))


def unpack_weight(words, scales, fmt):
    g, _, n = scales.shape
    words = np.ascontiguousarray(words).reshape(g, 128, n, -1)
    if fmt in ("e4m3", "e5m2"):
        vals = words.view(ml_dtypes.float8_e4m3fn if fmt == "e4m3" else ml_dtypes.float8_e5m2).astype(np.float64)
    else:
        nib = np.empty((g, 128, n, 4), np.uint8)
        nib[..., 0::2] = words & 0xF
        nib[..., 1::2] = words >> 4
        vals = E2M1[nib]
    vals = vals * np.repeat(np.exp2(scales.astype(np.float64) - 127.0), 8, axis=1)[..., None]
    return vals.transpose(0, 1, 3, 2).reshape(g * 512, n)


K, T, J, R, C, D = 512, 2048, 256, 512, 512, 512


def setup_inputs():
    n = np.random.standard_normal
    idx = np.random.permutation(T)[:J]
    idx2 = np.random.permutation(T)[:J]
    idx3 = np.stack([np.random.permutation(C)[:J] for _ in range(8)])
    idx4 = np.stack([np.random.permutation(D)[:J] for _ in range(8)])
    fk = mx_kscale(K)
    fr = mx_kscale(R)
    xtp = pack_weight(n((K, T)) / fk[:, None], "e2m1")
    wp = pack_weight(n((K, R)) * 1 / np.sqrt(K) * fk[:, None] * fr, "e4m3")
    w2p = pack_weight(n((K, R)) * 1 / np.sqrt(K) * fk[:, None] / fr, "e5m2")
    return {
        "xt_words": xtp[0],
        "xt_scales": xtp[1],
        "w_words": wp[0],
        "w_scales": wp[1],
        "w2_words": w2p[0],
        "w2_scales": w2p[1],
        "offs": striped(idx),
        "offs2": striped(idx2),
        "offs3": striped8(idx3),
        "offs4": striped8(idx4),
    }


def reference(xt_words, xt_scales, w_words, w_scales, w2_words, w2_scales, offs, offs2, offs3, offs4):
    idx = unstriped(offs)
    idx2 = unstriped(offs2)
    idx3 = unstriped8(offs3)
    idx4 = unstriped8(offs4)
    xtu = unpack_weight(xt_words, xt_scales, "e2m1")
    wu = unpack_weight(w_words, w_scales, "e4m3")
    w2u = unpack_weight(w2_words, w2_scales, "e5m2")
    xtidxg = xtu[:, idx]
    a = wu.T @ xtidxg
    xtidx2g = xtu[:, idx2]
    b = w2u.T @ xtidx2g
    pa = np.zeros((R, C))
    pa[np.arange(R)[:, None], idx3[np.arange(R) % 512 // 64]] = a
    pb = np.zeros((R, D))
    pb[np.arange(R)[:, None], idx4[np.arange(R) % 512 // 64]] = b
    paq = mxq(pa, 0, "e4m3")
    pbq = mxq(pb, 0, "e4m3")
    p = paq.T @ pbq
    return p

@@ -1,0 +1,161 @@
+from contextlib import ExitStack
+
+import concourse.mybir as mybir
+
+K, T, J, R, C, D = 512, 2048, 256, 512, 512, 512
+FLOPS = 2 * (2 * K * R * J) + 2 * R * C * D
+
+F32 = mybir.dt.float32
+BF16 = mybir.dt.bfloat16
+I32 = mybir.dt.int32
+U16 = mybir.dt.uint16
+U8 = mybir.dt.uint8
+E4M3 = mybir.dt.float8_e4m3fn_x4
+E5M2 = mybir.dt.float8_e5m2_x4
+E2M1 = mybir.dt.float4_e2m1fn_x4
+COPY = mybir.ActivationFunctionType.Copy
+
+P = 128
+SLOTS = 4
+QUADS = 4
+QUAD = 32
+RUN = 8
+CHUNKS = C // P
+
+
+def tile_list_boardsproduct_kernel(
+    tc, xt_words, xt_scales, w_words, w_scales, w2_words, w2_scales, offs, offs2, offs3, offs4, out
+):
+    nc = tc.nc
+    with ExitStack() as ctx:
+        lists = ctx.enter_context(tc.tile_pool(name="lists", bufs=1))
+        keep = ctx.enter_context(tc.tile_pool(name="keep", bufs=1))
+        psum = ctx.enter_context(tc.psum_pool(name="psum", bufs=8))
+
+        def load_list(src, name):
+            tile = lists.tile([P, J // 16], U16, name=name)
+            nc.sync.dma_start(tile[:], src)
+            return tile
+
+        def load_weight(queue, words, scales, name):
+            staged = keep.tile([QUADS, QUADS, R // 4], I32, name=name + "_staged")
+            queue.dma_start(staged[:], scales[0].bitcast(I32).rearrange("(q r) c -> r q c", r=4))
+            raw = keep.tile([P, R], I32, name=name + "_raw")
+            queue.dma_start(raw[:], words[0].rearrange("p n t -> p (n t)").bitcast(I32))
+            return raw, staged
+
+        def deal_scales(staged, name):
+            plane = keep.tile([P, R], U8, name=name + "_plane", align_bytes=64)
+            plane_words = plane[:].bitcast(I32)
+            nc.vector.memset(plane_words, 0)
+            for q in range(QUADS):
+                nc.vector.tensor_copy(
+                    plane_words[QUAD * q : QUAD * q + 4, :].rearrange("p (t g e) -> p t g e", t=SLOTS, e=2),
+                    staged[:, q, :].rearrange("p (g t e) -> p t g e", t=SLOTS, e=2),
+                )
+            return plane
+
+        def gather(index, name):
+            scales = keep.tile([P, J], U8, name=name + "_scales", align_bytes=64)
+            nc.vector.tensor_copy(scales[:], xs[:].indirect(index[:]))
+            words = keep.tile([P, J], U16, name=name + "_words", align_bytes=64)
+            nc.vector.tensor_copy(words[:], xw[:].indirect(index[:]))
+            return words, scales
+
+        def first_product(raw, plane, fmt, picked, name):
+            results = []
+            for t in range(SLOTS):
+                dealt = keep.tile([P, P], I32, name="%s_dealt%d" % (name, t), align_bytes=64)
+                nc.vector.tensor_copy(
+                    dealt[:].rearrange("p (g i) -> p g i", i=RUN),
+                    raw[:].rearrange("p (g t i) -> p t g i", t=SLOTS, i=RUN)[:, t],
+                )
+                acc = psum.tile([P, J], F32, name="acc")
+                nc.tensor.matmul_mx(
+                    acc[:],
+                    lhsT=dealt[:].bitcast(fmt),
+                    lhsT_scale=plane[:, t * P : (t + 1) * P],
+                    rhs=picked[0][:].bitcast(E2M1),
+                    rhs_scale=picked[1][:],
+                    start=True,
+                    stop=True,
+                )
+                result = keep.tile([P, J], F32, name="%s_result%d" % (name, t))
+                nc.vector.tensor_copy(result[:], acc[:])
+                results.append(result)
+            return results
+
+        def new_pages(name):
+            pages = []
+            for t in range(SLOTS):
+                page = keep.tile([P, C], F32, name="%s%d" % (name, t))
+                nc.vector.memset(page[:], 0.0)
+                pages.append(page)
+            return pages
+
+        xs = keep.tile([P, T], U8, name="xs")
+        nc.vector.memset(xs[:].bitcast(I32), 0)
+        list2 = load_list(offs2, "list2")
+        xw = keep.tile([P, T], U16, name="xw")
+        nc.scalar.dma_start(xw[:].bitcast(I32), xt_words[0].bitcast(I32))
+        w2_raw, w2_staged = load_weight(nc.scalar, w2_words, w2_scales, "w2")
+        for r in range(4):
+            nc.sync.dma_start(xs[:].bitcast(I32)[r:P:QUAD, :], xt_scales[0].bitcast(I32)[r:16:4, :])
+        list4 = load_list(offs4, "list4")
+        list1 = load_list(offs, "list1")
+        w_raw, w_staged = load_weight(nc.sync, w_words, w_scales, "w")
+        list3 = load_list(offs3, "list3")
+
+        w2_plane = deal_scales(w2_staged, "w2")
+        pb = new_pages("pb")
+        b = first_product(w2_raw, w2_plane, E5M2, gather(list2, "x2"), "b")
+        for t in range(SLOTS):
+            nc.scalar.activation(pb[t][:].indirect(list4[:]), b[t][:], COPY)
+
+        w_plane = deal_scales(w_staged, "w")
+        a = first_product(w_raw, w_plane, E4M3, gather(list1, "x1"), "a")
+        pa = new_pages("pa")
+
+        pb_woven = keep.tile([P, D, SLOTS], BF16, name="pb_woven", align_bytes=64)
+        for t in range(SLOTS):
+            nc.vector.tensor_copy(pb_woven[:, :, t], pb[t][:])
+        pb_codes = keep.tile([P, D], I32, name="pb_codes", align_bytes=64)
+        pb_scales = keep.tile([P, D], U8, name="pb_scales", align_bytes=64)
+        nc.vector.quantize_mx(pb_codes[:].bitcast(E4M3), pb_scales[:], pb_woven[:].rearrange("p d t -> p (d t)"))
+
+        pa_woven = [keep.tile([P, P, SLOTS], BF16, name="pa_woven%d" % c, align_bytes=64) for c in range(CHUNKS)]
+
+        def weave(t, c):
+            nc.vector.tensor_copy(pa_woven[c][:, :, t], pa[t][:, c * P : (c + 1) * P])
+
+        def finish(c):
+            codes = keep.tile([P, P], I32, name="pa_codes%d" % c, align_bytes=64)
+            scales = keep.tile([P, P], U8, name="pa_scales%d" % c, align_bytes=64)
+            nc.vector.quantize_mx(codes[:].bitcast(E4M3), scales[:], pa_woven[c][:].rearrange("p d t -> p (d t)"))
+            acc = psum.tile([P, D], F32, name="acc")
+            nc.tensor.matmul_mx(
+                acc[:],
+                lhsT=codes[:].bitcast(E4M3),
+                lhsT_scale=scales[:],
+                rhs=pb_codes[:].bitcast(E4M3),
+                rhs_scale=pb_scales[:],
+                start=True,
+                stop=True,
+            )
+            rows = keep.tile([P, D], F32, name="rows%d" % c)
+            if c == CHUNKS - 1:
+                nc.vector.tensor_copy(rows[:], acc[:])
+            else:
+                nc.scalar.copy(rows[:], acc[:])
+            nc.sync.dma_start(out[c * P : (c + 1) * P, :], rows[:])
+
+        for t in range(SLOTS):
+            nc.scalar.activation(pa[t][:].indirect(list3[:]), a[t][:], COPY)
+            if t < SLOTS - 1:
+                for c in range(CHUNKS):
+                    weave(t, c)
+        weave(SLOTS - 1, 0)
+        for c in range(CHUNKS):
+            if c + 1 < CHUNKS:
+                weave(SLOTS - 1, c + 1)
+            finish(c)

@@ -21,6 +21,8 @@ QUADS = 4
 QUAD = 32
 RUN = 8
 CHUNKS = C // P
+HALF = D // 2
+LAST = SLOTS - 1
 
 
 def tile_list_boardsproduct_kernel(
@@ -37,12 +39,15 @@ def tile_list_boardsproduct_kernel(
             nc.sync.dma_start(tile[:], src)
             return tile
 
-        def load_weight(queue, words, scales, name):
-            staged = keep.tile([QUADS, QUADS, R // 4], I32, name=name + "_staged")
+        def load_scales(queue, scales, name):
+            staged = keep.tile([QUADS, QUADS, R // 4], I32, name=name + "_staged", tag="staged")
             queue.dma_start(staged[:], scales[0].bitcast(I32).rearrange("(q r) c -> r q c", r=4))
-            raw = keep.tile([P, R], I32, name=name + "_raw")
-            queue.dma_start(raw[:], words[0].rearrange("p n t -> p (n t)").bitcast(I32))
-            return raw, staged
+            return staged
+
+        def load_words(words, name):
+            raw = keep.tile([P, R], I32, name=name + "_raw", tag=name + "_raw")
+            nc.sync.dma_start(raw[:], words[0].rearrange("p n t -> p (n t)").bitcast(I32))
+            return raw
 
         def deal_scales(staged, name):
             plane = keep.tile([P, R], U8, name=name + "_plane", align_bytes=64)
@@ -56,10 +61,10 @@ def tile_list_boardsproduct_kernel(
             return plane
 
         def gather(index, name):
+            words = keep.tile([P, J], U16, name=name + "_words", tag=name + "_words", align_bytes=64)
+            nc.vector.tensor_copy(words[:], xw[:].indirect(index[:]))
             scales = keep.tile([P, J], U8, name=name + "_scales", align_bytes=64)
             nc.vector.tensor_copy(scales[:], xs[:].indirect(index[:]))
-            words = keep.tile([P, J], U16, name=name + "_words", align_bytes=64)
-            nc.vector.tensor_copy(words[:], xw[:].indirect(index[:]))
             return words, scales
 
         def first_product(raw, plane, fmt, picked, name):
@@ -81,81 +86,97 @@ def tile_list_boardsproduct_kernel(
                     stop=True,
                 )
                 result = keep.tile([P, J], F32, name="%s_result%d" % (name, t))
-                nc.vector.tensor_copy(result[:], acc[:])
+                if name == "b" and t == 0:
+                    nc.scalar.activation(result[:], acc[:], COPY)
+                else:
+                    nc.vector.tensor_copy(result[:], acc[:])
                 results.append(result)
             return results
 
-        def new_pages(name):
+        def new_pages(name, tags, engines):
             pages = []
             for t in range(SLOTS):
-                page = keep.tile([P, C], F32, name="%s%d" % (name, t))
-                nc.vector.memset(page[:], 0.0)
+                page = keep.tile([P, C], F32, name="%s%d" % (name, t), tag=tags[t])
+                engines[t].memset(page[:], 0.0)
                 pages.append(page)
             return pages
 
-        xs = keep.tile([P, T], U8, name="xs")
+        xs = keep.tile([P, T], U8, name="xs", tag="xs")
         nc.vector.memset(xs[:].bitcast(I32), 0)
         list2 = load_list(offs2, "list2")
-        xw = keep.tile([P, T], U16, name="xw")
-        nc.scalar.dma_start(xw[:].bitcast(I32), xt_words[0].bitcast(I32))
-        w2_raw, w2_staged = load_weight(nc.scalar, w2_words, w2_scales, "w2")
+        xw = keep.tile([P, T], U16, name="xw", tag="xw")
+        w2_staged = load_scales(nc.scalar, w2_scales, "w2")
+        nc.sync.dma_start(xw[:].bitcast(I32), xt_words[0].bitcast(I32))
         for r in range(4):
             nc.sync.dma_start(xs[:].bitcast(I32)[r:P:QUAD, :], xt_scales[0].bitcast(I32)[r:16:4, :])
+        w2_raw = load_words(w2_words, "w2")
         list4 = load_list(offs4, "list4")
         list1 = load_list(offs, "list1")
-        w_raw, w_staged = load_weight(nc.sync, w_words, w_scales, "w")
+        w_raw = load_words(w_words, "w")
         list3 = load_list(offs3, "list3")
 
         w2_plane = deal_scales(w2_staged, "w2")
-        pb = new_pages("pb")
+        pb = new_pages("pb", ["pb0", "pb1", "pb2", "pb3"], [nc.vector, nc.vector, nc.gpsimd, nc.gpsimd])
         b = first_product(w2_raw, w2_plane, E5M2, gather(list2, "x2"), "b")
         for t in range(SLOTS):
             nc.scalar.activation(pb[t][:].indirect(list4[:]), b[t][:], COPY)
 
-        w_plane = deal_scales(w_staged, "w")
+        w_plane = deal_scales(load_scales(nc.sync, w_scales, "w"), "w")
         a = first_product(w_raw, w_plane, E4M3, gather(list1, "x1"), "a")
-        pa = new_pages("pa")
+        pa = new_pages("pa", ["w2_raw", "xw", "xs", "w_raw"], [nc.vector] * SLOTS)
 
         pb_woven = keep.tile([P, D, SLOTS], BF16, name="pb_woven", align_bytes=64)
+        pb_rounded = keep.tile([P, SLOTS, D], BF16, name="pb_rounded", tag="x1_words", align_bytes=64)
         for t in range(SLOTS):
-            nc.vector.tensor_copy(pb_woven[:, :, t], pb[t][:])
+            nc.vector.tensor_copy(pb_rounded[:, t, :], pb[t][:])
+        nc.vector.tensor_copy(pb_woven[:], pb_rounded[:].rearrange("p t d -> p d t"))
         pb_codes = keep.tile([P, D], I32, name="pb_codes", align_bytes=64)
         pb_scales = keep.tile([P, D], U8, name="pb_scales", align_bytes=64)
         nc.vector.quantize_mx(pb_codes[:].bitcast(E4M3), pb_scales[:], pb_woven[:].rearrange("p d t -> p (d t)"))
 
-        pa_woven = [keep.tile([P, P, SLOTS], BF16, name="pa_woven%d" % c, align_bytes=64) for c in range(CHUNKS)]
+        pa_woven = {}
 
-        def weave(t, c):
-            nc.vector.tensor_copy(pa_woven[c][:, :, t], pa[t][:, c * P : (c + 1) * P])
+        def weave_first(c):
+            pa_woven[c] = keep.tile([P, P, SLOTS], BF16, name="pa_woven%d" % c, tag="pa_woven%d" % (c % 2), align_bytes=64)
+            nc.vector.tensor_copy(
+                pa_woven[c][:, :, 0:LAST], pa_rounded[:, :, c * P : (c + 1) * P].rearrange("p t c -> p c t")
+            )
+
+        def weave_last(c):
+            nc.vector.tensor_copy(pa_woven[c][:, :, LAST], pa[LAST][:, c * P : (c + 1) * P])
 
         def finish(c):
             codes = keep.tile([P, P], I32, name="pa_codes%d" % c, align_bytes=64)
             scales = keep.tile([P, P], U8, name="pa_scales%d" % c, align_bytes=64)
             nc.vector.quantize_mx(codes[:].bitcast(E4M3), scales[:], pa_woven[c][:].rearrange("p d t -> p (d t)"))
-            acc = psum.tile([P, D], F32, name="acc")
-            nc.tensor.matmul_mx(
-                acc[:],
-                lhsT=codes[:].bitcast(E4M3),
-                lhsT_scale=scales[:],
-                rhs=pb_codes[:].bitcast(E4M3),
-                rhs_scale=pb_scales[:],
-                start=True,
-                stop=True,
-            )
-            rows = keep.tile([P, D], F32, name="rows%d" % c)
-            if c == CHUNKS - 1:
-                nc.vector.tensor_copy(rows[:], acc[:])
-            else:
-                nc.scalar.copy(rows[:], acc[:])
-            nc.sync.dma_start(out[c * P : (c + 1) * P, :], rows[:])
+            for h in range(2):
+                cols = slice(h * HALF, (h + 1) * HALF)
+                acc = psum.tile([P, HALF], F32, name="acc")
+                nc.tensor.matmul_mx(
+                    acc[:],
+                    lhsT=codes[:].bitcast(E4M3),
+                    lhsT_scale=scales[:],
+                    rhs=pb_codes[:, cols].bitcast(E4M3),
+                    rhs_scale=pb_scales[:, cols],
+                    start=True,
+                    stop=True,
+                )
+                rows = keep.tile([P, HALF], F32, name="rows%d_%d" % (c, h))
+                if c == CHUNKS - 1 and h == 1:
+                    nc.vector.tensor_copy(rows[:], acc[:])
+                else:
+                    nc.scalar.copy(rows[:], acc[:])
+                nc.sync.dma_start(out[c * P : (c + 1) * P, cols], rows[:])
 
+        pa_rounded = keep.tile([P, LAST, C], BF16, name="pa_rounded")
         for t in range(SLOTS):
             nc.scalar.activation(pa[t][:].indirect(list3[:]), a[t][:], COPY)
-            if t < SLOTS - 1:
-                for c in range(CHUNKS):
-                    weave(t, c)
-        weave(SLOTS - 1, 0)
-        for c in range(CHUNKS):
-            if c + 1 < CHUNKS:
-                weave(SLOTS - 1, c + 1)
-            finish(c)
+            if t < LAST:
+                nc.vector.tensor_copy(pa_rounded[:, t, :], pa[t][:])
+        for pair in ((0, 1), (2, 3)):
+            for c in pair:
+                weave_first(c)
+            for c in pair:
+                weave_last(c)
+            for c in pair:
+                finish(c)

@@ -45,7 +45,7 @@ def tile_list_boardsproduct_kernel(
             return staged
 
         def load_words(words, name):
-            raw = keep.tile([P, R], I32, name=name + "_raw", tag=name + "_raw")
+            raw = keep.tile([P, R], I32, name=name + "_raw", tag=name + "_raw", align_bytes=64)
             nc.sync.dma_start(raw[:], words[0].rearrange("p n t -> p (n t)").bitcast(I32))
             return raw
 
@@ -70,41 +70,45 @@ def tile_list_boardsproduct_kernel(
         def first_product(raw, plane, fmt, picked, name):
             results = []
             for t in range(SLOTS):
-                dealt = keep.tile([P, P], I32, name="%s_dealt%d" % (name, t), align_bytes=64)
+                dealt = keep.tile([P, P], I32, name="%s_dealt%d" % (name, t), tag="%s_dealt%d" % (name, t), align_bytes=64)
                 nc.vector.tensor_copy(
                     dealt[:].rearrange("p (g i) -> p g i", i=RUN),
                     raw[:].rearrange("p (g t i) -> p t g i", t=SLOTS, i=RUN)[:, t],
                 )
-                acc = psum.tile([P, J], F32, name="acc")
-                nc.tensor.matmul_mx(
-                    acc[:],
-                    lhsT=dealt[:].bitcast(fmt),
-                    lhsT_scale=plane[:, t * P : (t + 1) * P],
-                    rhs=picked[0][:].bitcast(E2M1),
-                    rhs_scale=picked[1][:],
-                    start=True,
-                    stop=True,
-                )
                 result = keep.tile([P, J], F32, name="%s_result%d" % (name, t))
-                if name == "b" and t == 0:
-                    nc.scalar.activation(result[:], acc[:], COPY)
-                else:
-                    nc.vector.tensor_copy(result[:], acc[:])
+                first = name == "b" and t == 0
+                width = J // 2 if first else J
+                for j0 in range(0, J, width):
+                    cols = slice(j0, j0 + width)
+                    acc = psum.tile([P, width], F32, name="acc")
+                    nc.tensor.matmul_mx(
+                        acc[:],
+                        lhsT=dealt[:].bitcast(fmt),
+                        lhsT_scale=plane[:, t * P : (t + 1) * P],
+                        rhs=picked[0][:, cols].bitcast(E2M1),
+                        rhs_scale=picked[1][:, cols],
+                        start=True,
+                        stop=True,
+                    )
+                    if first and j0 == 0:
+                        nc.scalar.activation(result[:, cols], acc[:], COPY)
+                    else:
+                        nc.vector.tensor_copy(result[:, cols], acc[:])
                 results.append(result)
             return results
 
         def new_pages(name, tags, engines):
             pages = []
             for t in range(SLOTS):
-                page = keep.tile([P, C], F32, name="%s%d" % (name, t), tag=tags[t])
+                page = keep.tile([P, C], F32, name="%s%d" % (name, t), tag=tags[t], align_bytes=64)
                 engines[t].memset(page[:], 0.0)
                 pages.append(page)
             return pages
 
-        xs = keep.tile([P, T], U8, name="xs", tag="xs")
+        xs = keep.tile([P, T], U8, name="xs")
         nc.vector.memset(xs[:].bitcast(I32), 0)
         list2 = load_list(offs2, "list2")
-        xw = keep.tile([P, T], U16, name="xw", tag="xw")
+        xw = keep.tile([P, T], U16, name="xw")
         w2_staged = load_scales(nc.scalar, w2_scales, "w2")
         nc.sync.dma_start(xw[:].bitcast(I32), xt_words[0].bitcast(I32))
         for r in range(4):
@@ -118,12 +122,15 @@ def tile_list_boardsproduct_kernel(
         w2_plane = deal_scales(w2_staged, "w2")
         pb = new_pages("pb", ["pb0", "pb1", "pb2", "pb3"], [nc.vector, nc.vector, nc.gpsimd, nc.gpsimd])
         b = first_product(w2_raw, w2_plane, E5M2, gather(list2, "x2"), "b")
-        for t in range(SLOTS):
+        nc.scalar.activation(pb[0][:].indirect(list4[:, 0:8]), b[0][:, 0:P], COPY)
+        nc.scalar.activation(pb[1][:].indirect(list4[:]), b[1][:], COPY)
+        nc.scalar.activation(pb[0][:].indirect(list4[:, 8:16]), b[0][:, P:J], COPY)
+        for t in range(2, SLOTS):
             nc.scalar.activation(pb[t][:].indirect(list4[:]), b[t][:], COPY)
 
         w_plane = deal_scales(load_scales(nc.sync, w_scales, "w"), "w")
         a = first_product(w_raw, w_plane, E4M3, gather(list1, "x1"), "a")
-        pa = new_pages("pa", ["w2_raw", "xw", "xs", "w_raw"], [nc.vector] * SLOTS)
+        pa = new_pages("pa", ["w2_raw", "w_raw", "a_dealt0", "a_dealt1"], [nc.vector] * SLOTS)
 
         pb_woven = keep.tile([P, D, SLOTS], BF16, name="pb_woven", align_bytes=64)
         pb_rounded = keep.tile([P, SLOTS, D], BF16, name="pb_rounded", tag="x1_words", align_bytes=64)
@@ -134,24 +141,29 @@ def tile_list_boardsproduct_kernel(
         pb_scales = keep.tile([P, D], U8, name="pb_scales", align_bytes=64)
         nc.vector.quantize_mx(pb_codes[:].bitcast(E4M3), pb_scales[:], pb_woven[:].rearrange("p d t -> p (d t)"))
 
-        pa_woven = {}
+        pa_rounded = keep.tile([P, SLOTS, C], BF16, name="pa_rounded")
+        for t in range(SLOTS):
+            nc.scalar.activation(pa[t][:].indirect(list3[:]), a[t][:], COPY)
+            if t < LAST:
+                nc.vector.tensor_copy(pa_rounded[:, t, :], pa[t][:])
 
-        def weave_first(c):
-            pa_woven[c] = keep.tile([P, P, SLOTS], BF16, name="pa_woven%d" % c, tag="pa_woven%d" % (c % 2), align_bytes=64)
-            nc.vector.tensor_copy(
-                pa_woven[c][:, :, 0:LAST], pa_rounded[:, :, c * P : (c + 1) * P].rearrange("p t c -> p c t")
-            )
+        def woven_tile(c, tag):
+            return keep.tile([P, P, SLOTS], BF16, name="pa_woven%d" % c, tag=tag, align_bytes=64)
 
-        def weave_last(c):
-            nc.vector.tensor_copy(pa_woven[c][:, :, LAST], pa[LAST][:, c * P : (c + 1) * P])
+        def rounded(c, slots):
+            return pa_rounded[:, 0:slots, c * P : (c + 1) * P].rearrange("p t c -> p c t")
 
-        def finish(c):
+        def quantise(c, woven):
             codes = keep.tile([P, P], I32, name="pa_codes%d" % c, align_bytes=64)
             scales = keep.tile([P, P], U8, name="pa_scales%d" % c, align_bytes=64)
-            nc.vector.quantize_mx(codes[:].bitcast(E4M3), scales[:], pa_woven[c][:].rearrange("p d t -> p (d t)"))
-            for h in range(2):
-                cols = slice(h * HALF, (h + 1) * HALF)
-                acc = psum.tile([P, HALF], F32, name="acc")
+            nc.vector.quantize_mx(codes[:].bitcast(E4M3), scales[:], woven[:].rearrange("p c t -> p (c t)"))
+            return codes, scales
+
+        def product(c, codes, scales):
+            starts = [0, P, HALF, D] if c == 0 else [0, HALF, D]
+            for d0, d1 in zip(starts, starts[1:]):
+                cols = slice(d0, d1)
+                acc = psum.tile([P, d1 - d0], F32, name="acc")
                 nc.tensor.matmul_mx(
                     acc[:],
                     lhsT=codes[:].bitcast(E4M3),
@@ -161,22 +173,24 @@ def tile_list_boardsproduct_kernel(
                     start=True,
                     stop=True,
                 )
-                rows = keep.tile([P, HALF], F32, name="rows%d_%d" % (c, h))
-                if c == CHUNKS - 1 and h == 1:
+                rows = keep.tile([P, d1 - d0], F32, name="rows%d_%d" % (c, d0))
+                if c >= 2 and d0 == HALF:
                     nc.vector.tensor_copy(rows[:], acc[:])
                 else:
                     nc.scalar.copy(rows[:], acc[:])
                 nc.sync.dma_start(out[c * P : (c + 1) * P, cols], rows[:])
 
-        pa_rounded = keep.tile([P, LAST, C], BF16, name="pa_rounded")
-        for t in range(SLOTS):
-            nc.scalar.activation(pa[t][:].indirect(list3[:]), a[t][:], COPY)
-            if t < LAST:
-                nc.vector.tensor_copy(pa_rounded[:, t, :], pa[t][:])
-        for pair in ((0, 1), (2, 3)):
-            for c in pair:
-                weave_first(c)
-            for c in pair:
-                weave_last(c)
-            for c in pair:
-                finish(c)
+        early = [woven_tile(c, "woven%d" % c) for c in range(2)]
+        for c in range(2):
+            nc.vector.tensor_copy(early[c][:, :, 0:LAST], rounded(c, LAST))
+        for c in range(2):
+            nc.vector.tensor_copy(early[c][:, :, LAST], pa[LAST][:, c * P : (c + 1) * P])
+        quantised = [quantise(c, early[c]) for c in range(2)]
+
+        nc.scalar.copy(pa_rounded[:, LAST, 2 * P :], pa[LAST][:, 2 * P :])
+        late = [woven_tile(c, "woven%d" % (c - 2)) for c in range(2, CHUNKS)]
+        for c in range(2, CHUNKS):
+            nc.vector.tensor_copy(late[c - 2][:], rounded(c, SLOTS))
+        quantised += [quantise(c, late[c - 2]) for c in range(2, CHUNKS)]
+        for c in range(CHUNKS):
+            product(c, *quantised[c])

@@ -49,8 +49,8 @@ def tile_list_boardsproduct_kernel(
             nc.sync.dma_start(raw[:], words[0].rearrange("p n t -> p (n t)").bitcast(I32))
             return raw
 
-        def deal_scales(staged, name):
-            plane = keep.tile([P, R], U8, name=name + "_plane", align_bytes=64)
+        def deal_scales(staged, name, tag):
+            plane = keep.tile([P, R], U8, name=name + "_plane", tag=tag, align_bytes=64)
             plane_words = plane[:].bitcast(I32)
             nc.vector.memset(plane_words, 0)
             for q in range(QUADS):
@@ -60,10 +60,10 @@ def tile_list_boardsproduct_kernel(
                 )
             return plane
 
-        def gather(index, name):
-            words = keep.tile([P, J], U16, name=name + "_words", tag=name + "_words", align_bytes=64)
+        def gather(index, name, words_tag, scales_tag):
+            words = keep.tile([P, J], U16, name=name + "_words", tag=words_tag, align_bytes=64)
             nc.vector.tensor_copy(words[:], xw[:].indirect(index[:]))
-            scales = keep.tile([P, J], U8, name=name + "_scales", align_bytes=64)
+            scales = keep.tile([P, J], U8, name=name + "_scales", tag=scales_tag, align_bytes=64)
             nc.vector.tensor_copy(scales[:], xs[:].indirect(index[:]))
             return words, scales
 
@@ -90,7 +90,7 @@ def tile_list_boardsproduct_kernel(
                         start=True,
                         stop=True,
                     )
-                    if first and j0 == 0:
+                    if first and j0 > 0:
                         nc.scalar.activation(result[:, cols], acc[:], COPY)
                     else:
                         nc.vector.tensor_copy(result[:, cols], acc[:])
@@ -119,21 +119,21 @@ def tile_list_boardsproduct_kernel(
         w_raw = load_words(w_words, "w")
         list3 = load_list(offs3, "list3")
 
-        w2_plane = deal_scales(w2_staged, "w2")
+        w2_plane = deal_scales(w2_staged, "w2", "w2_plane")
         pb = new_pages("pb", ["pb0", "pb1", "pb2", "pb3"], [nc.vector, nc.vector, nc.gpsimd, nc.gpsimd])
-        b = first_product(w2_raw, w2_plane, E5M2, gather(list2, "x2"), "b")
+        b = first_product(w2_raw, w2_plane, E5M2, gather(list2, "x2", "x2_words", "x2_scales"), "b")
         nc.scalar.activation(pb[0][:].indirect(list4[:, 0:8]), b[0][:, 0:P], COPY)
         nc.scalar.activation(pb[1][:].indirect(list4[:]), b[1][:], COPY)
         nc.scalar.activation(pb[0][:].indirect(list4[:, 8:16]), b[0][:, P:J], COPY)
         for t in range(2, SLOTS):
             nc.scalar.activation(pb[t][:].indirect(list4[:]), b[t][:], COPY)
 
-        w_plane = deal_scales(load_scales(nc.sync, w_scales, "w"), "w")
-        a = first_product(w_raw, w_plane, E4M3, gather(list1, "x1"), "a")
-        pa = new_pages("pa", ["w2_raw", "w_raw", "a_dealt0", "a_dealt1"], [nc.vector] * SLOTS)
+        w_plane = deal_scales(load_scales(nc.sync, w_scales, "w"), "w", "b_dealt1")
+        a = first_product(w_raw, w_plane, E4M3, gather(list1, "x1", "b_dealt3", "b_dealt2"), "a")
+        pa = new_pages("pa", ["x2_words", "w_raw", "a_dealt0", "a_dealt1"], [nc.vector] * SLOTS)
 
         pb_woven = keep.tile([P, D, SLOTS], BF16, name="pb_woven", align_bytes=64)
-        pb_rounded = keep.tile([P, SLOTS, D], BF16, name="pb_rounded", tag="x1_words", align_bytes=64)
+        pb_rounded = keep.tile([P, SLOTS, D], BF16, name="pb_rounded", tag="b_dealt3", align_bytes=64)
         for t in range(SLOTS):
             nc.vector.tensor_copy(pb_rounded[:, t, :], pb[t][:])
         nc.vector.tensor_copy(pb_woven[:], pb_rounded[:].rearrange("p t d -> p d t"))

from contextlib import ExitStack

import concourse.mybir as mybir

K, T, J, R, C, D = 512, 2048, 256, 512, 512, 512
FLOPS = 2 * (2 * K * R * J) + 2 * R * C * D

F32 = mybir.dt.float32
BF16 = mybir.dt.bfloat16
I32 = mybir.dt.int32
U16 = mybir.dt.uint16
U8 = mybir.dt.uint8
E4M3 = mybir.dt.float8_e4m3fn_x4
E5M2 = mybir.dt.float8_e5m2_x4
E2M1 = mybir.dt.float4_e2m1fn_x4
COPY = mybir.ActivationFunctionType.Copy

P = 128
SLOTS = 4
QUADS = 4
QUAD = 32
RUN = 8
CHUNKS = C // P
HALF = D // 2
LAST = SLOTS - 1


def tile_list_boardsproduct_kernel(
    tc, xt_words, xt_scales, w_words, w_scales, w2_words, w2_scales, offs, offs2, offs3, offs4, out
):
    nc = tc.nc
    with ExitStack() as ctx:
        lists = ctx.enter_context(tc.tile_pool(name="lists", bufs=1))
        keep = ctx.enter_context(tc.tile_pool(name="keep", bufs=1))
        psum = ctx.enter_context(tc.psum_pool(name="psum", bufs=8))

        def load_list(src, name):
            tile = lists.tile([P, J // 16], U16, name=name)
            nc.sync.dma_start(tile[:], src)
            return tile

        def load_scales(queue, scales, name):
            staged = keep.tile([QUADS, QUADS, R // 4], I32, name=name + "_staged", tag="staged")
            queue.dma_start(staged[:], scales[0].bitcast(I32).rearrange("(q r) c -> r q c", r=4))
            return staged

        def load_words(words, name):
            raw = keep.tile([P, R], I32, name=name + "_raw", tag=name + "_raw", align_bytes=64)
            nc.sync.dma_start(raw[:], words[0].rearrange("p n t -> p (n t)").bitcast(I32))
            return raw

        def deal_scales(staged, name, tag):
            plane = keep.tile([P, R], U8, name=name + "_plane", tag=tag, align_bytes=64)
            plane_words = plane[:].bitcast(I32)
            nc.vector.memset(plane_words, 0)
            for q in range(QUADS):
                nc.vector.tensor_copy(
                    plane_words[QUAD * q : QUAD * q + 4, :].rearrange("p (t g e) -> p t g e", t=SLOTS, e=2),
                    staged[:, q, :].rearrange("p (g t e) -> p t g e", t=SLOTS, e=2),
                )
            return plane

        def gather(index, name, words_tag, scales_tag):
            words = keep.tile([P, J], U16, name=name + "_words", tag=words_tag, align_bytes=64)
            nc.vector.tensor_copy(words[:], xw[:].indirect(index[:]))
            scales = keep.tile([P, J], U8, name=name + "_scales", tag=scales_tag, align_bytes=64)
            nc.vector.tensor_copy(scales[:], xs[:].indirect(index[:]))
            return words, scales

        def first_product(raw, plane, fmt, picked, name):
            results = []
            for t in range(SLOTS):
                dealt = keep.tile([P, P], I32, name="%s_dealt%d" % (name, t), tag="%s_dealt%d" % (name, t), align_bytes=64)
                nc.vector.tensor_copy(
                    dealt[:].rearrange("p (g i) -> p g i", i=RUN),
                    raw[:].rearrange("p (g t i) -> p t g i", t=SLOTS, i=RUN)[:, t],
                )
                result = keep.tile([P, J], F32, name="%s_result%d" % (name, t))
                first = name == "b" and t == 0
                width = J // 2 if first else J
                for j0 in range(0, J, width):
                    cols = slice(j0, j0 + width)
                    acc = psum.tile([P, width], F32, name="acc")
                    nc.tensor.matmul_mx(
                        acc[:],
                        lhsT=dealt[:].bitcast(fmt),
                        lhsT_scale=plane[:, t * P : (t + 1) * P],
                        rhs=picked[0][:, cols].bitcast(E2M1),
                        rhs_scale=picked[1][:, cols],
                        start=True,
                        stop=True,
                    )
                    if first and j0 > 0:
                        nc.scalar.activation(result[:, cols], acc[:], COPY)
                    else:
                        nc.vector.tensor_copy(result[:, cols], acc[:])
                results.append(result)
            return results

        def new_pages(name, tags, engines):
            pages = []
            for t in range(SLOTS):
                page = keep.tile([P, C], F32, name="%s%d" % (name, t), tag=tags[t], align_bytes=64)
                engines[t].memset(page[:], 0.0)
                pages.append(page)
            return pages

        xs = keep.tile([P, T], U8, name="xs")
        nc.vector.memset(xs[:].bitcast(I32), 0)
        list2 = load_list(offs2, "list2")
        xw = keep.tile([P, T], U16, name="xw")
        w2_staged = load_scales(nc.scalar, w2_scales, "w2")
        nc.sync.dma_start(xw[:].bitcast(I32), xt_words[0].bitcast(I32))
        for r in range(4):
            nc.sync.dma_start(xs[:].bitcast(I32)[r:P:QUAD, :], xt_scales[0].bitcast(I32)[r:16:4, :])
        w2_raw = load_words(w2_words, "w2")
        list4 = load_list(offs4, "list4")
        list1 = load_list(offs, "list1")
        w_raw = load_words(w_words, "w")
        list3 = load_list(offs3, "list3")

        w2_plane = deal_scales(w2_staged, "w2", "w2_plane")
        pb = new_pages("pb", ["pb0", "pb1", "pb2", "pb3"], [nc.vector, nc.vector, nc.gpsimd, nc.gpsimd])
        b = first_product(w2_raw, w2_plane, E5M2, gather(list2, "x2", "x2_words", "x2_scales"), "b")
        nc.scalar.activation(pb[0][:].indirect(list4[:, 0:8]), b[0][:, 0:P], COPY)
        nc.scalar.activation(pb[1][:].indirect(list4[:]), b[1][:], COPY)
        nc.scalar.activation(pb[0][:].indirect(list4[:, 8:16]), b[0][:, P:J], COPY)
        for t in range(2, SLOTS):
            nc.scalar.activation(pb[t][:].indirect(list4[:]), b[t][:], COPY)

        w_plane = deal_scales(load_scales(nc.sync, w_scales, "w"), "w", "b_dealt1")
        a = first_product(w_raw, w_plane, E4M3, gather(list1, "x1", "b_dealt3", "b_dealt2"), "a")
        pa = new_pages("pa", ["x2_words", "w_raw", "a_dealt0", "a_dealt1"], [nc.vector] * SLOTS)

        pb_woven = keep.tile([P, D, SLOTS], BF16, name="pb_woven", align_bytes=64)
        pb_rounded = keep.tile([P, SLOTS, D], BF16, name="pb_rounded", tag="b_dealt3", align_bytes=64)
        for t in range(SLOTS):
            nc.vector.tensor_copy(pb_rounded[:, t, :], pb[t][:])
        nc.vector.tensor_copy(pb_woven[:], pb_rounded[:].rearrange("p t d -> p d t"))
        pb_codes = keep.tile([P, D], I32, name="pb_codes", align_bytes=64)
        pb_scales = keep.tile([P, D], U8, name="pb_scales", align_bytes=64)
        nc.vector.quantize_mx(pb_codes[:].bitcast(E4M3), pb_scales[:], pb_woven[:].rearrange("p d t -> p (d t)"))

        pa_rounded = keep.tile([P, SLOTS, C], BF16, name="pa_rounded")
        for t in range(SLOTS):
            nc.scalar.activation(pa[t][:].indirect(list3[:]), a[t][:], COPY)
            if t < LAST:
                nc.vector.tensor_copy(pa_rounded[:, t, :], pa[t][:])

        def woven_tile(c, tag):
            return keep.tile([P, P, SLOTS], BF16, name="pa_woven%d" % c, tag=tag, align_bytes=64)

        def rounded(c, slots):
            return pa_rounded[:, 0:slots, c * P : (c + 1) * P].rearrange("p t c -> p c t")

        def quantise(c, woven):
            codes = keep.tile([P, P], I32, name="pa_codes%d" % c, align_bytes=64)
            scales = keep.tile([P, P], U8, name="pa_scales%d" % c, align_bytes=64)
            nc.vector.quantize_mx(codes[:].bitcast(E4M3), scales[:], woven[:].rearrange("p c t -> p (c t)"))
            return codes, scales

        def product(c, codes, scales):
            starts = [0, P, HALF, D] if c == 0 else [0, HALF, D]
            for d0, d1 in zip(starts, starts[1:]):
                cols = slice(d0, d1)
                acc = psum.tile([P, d1 - d0], F32, name="acc")
                nc.tensor.matmul_mx(
                    acc[:],
                    lhsT=codes[:].bitcast(E4M3),
                    lhsT_scale=scales[:],
                    rhs=pb_codes[:, cols].bitcast(E4M3),
                    rhs_scale=pb_scales[:, cols],
                    start=True,
                    stop=True,
                )
                rows = keep.tile([P, d1 - d0], F32, name="rows%d_%d" % (c, d0))
                if c >= 2 and d0 == HALF:
                    nc.vector.tensor_copy(rows[:], acc[:])
                else:
                    nc.scalar.copy(rows[:], acc[:])
                nc.sync.dma_start(out[c * P : (c + 1) * P, cols], rows[:])

        early = [woven_tile(c, "woven%d" % c) for c in range(2)]
        for c in range(2):
            nc.vector.tensor_copy(early[c][:, :, 0:LAST], rounded(c, LAST))
        for c in range(2):
            nc.vector.tensor_copy(early[c][:, :, LAST], pa[LAST][:, c * P : (c + 1) * P])
        quantised = [quantise(c, early[c]) for c in range(2)]

        nc.scalar.copy(pa_rounded[:, LAST, 2 * P :], pa[LAST][:, 2 * P :])
        late = [woven_tile(c, "woven%d" % (c - 2)) for c in range(2, CHUNKS)]
        for c in range(2, CHUNKS):
            nc.vector.tensor_copy(late[c - 2][:], rounded(c, SLOTS))
        quantised += [quantise(c, late[c - 2]) for c in range(2, CHUNKS)]
        for c in range(CHUNKS):
            product(c, *quantised[c])
